import numpy as np
import ml_dtypes


def mxq(x, axis, fmt="e4m3"):
    dtype, down = {"e4m3": (ml_dtypes.float8_e4m3fn, 7), "e5m2": (ml_dtypes.float8_e5m2, 14)}[fmt]
    v = np.moveaxis(np.asarray(x, np.float32).astype(ml_dtypes.bfloat16).astype(np.float64), axis, -1)
    blocks = v.reshape(v.shape[:-1] + (-1, 32))
    amax = np.abs(blocks).max(-1, keepdims=True)
    byte = np.maximum(np.where(amax > 0, np.frexp(amax)[1] - 1 + 127, 0) - down, 1)
    scale = np.exp2(byte - 127.0)
    codes = (blocks / scale).astype(np.float32).astype(dtype).astype(np.float64)
    return np.moveaxis((codes * scale).reshape(v.shape), -1, axis)


WIDE = False


def mx_kscale(k):
    if not WIDE:
        return np.ones(k)
    levels = np.array([10, -10, 5, -5, 0])
    if k % 512:
        return np.exp2(np.random.permutation(np.resize(levels, k // 32))).repeat(32)
    a = np.empty((k // 512, 16))
    for p in range(k // 512):
        a[p, :8] = np.random.permutation(np.resize(levels, 8))
        for g in range(8):
            far = levels[np.abs(levels - a[p, g]) >= 10]
            a[p, g + 8] = far[np.random.randint(len(far))]
    return np.exp2(a.ravel()).repeat(32)


def f64(x):
    return np.asarray(x).astype(np.float64)


def striped(idx):
    return np.tile(idx.reshape(-1, 16).T, (8, 1)).astype(np.uint16)


def unstriped(offs):
    return offs[:16].T.reshape(-1).astype(np.int64)


E2M1 = np.array([0.0, 0.5, 1.0, 1.5, 2.0, 3.0, 4.0, 6.0, -0.0, -0.5, -1.0, -1.5, -2.0, -3.0, -4.0, -6.0])


def pack_weight(w, fmt):
    k, n = w.shape
    w = f64(np.asarray(w, np.float32).astype(ml_dtypes.bfloat16)).reshape(k // 32, 32, n)
    amax = np.abs(w).max(1)
    if fmt == "e4m3":
        byte = np.frexp(amax)[1] - 1 + 127 - 7
    else:
        mant, ex = np.frexp(amax / 6.0)
        byte = np.where(mant > 0.5, ex, ex - 1) + 127
    byte = np.clip(np.where(amax > 0, byte, 1), 1, 254)
    scaled = (w * np.exp2(127.0 - byte)[:, None, :]).reshape(k, n).astype(np.float32)
    by_word = np.ascontiguousarray(scaled.reshape(k // 512, 128, 4, n).transpose(0, 1, 3, 2))
    if fmt == "e4m3":
        words = by_word.astype(ml_dtypes.float8_e4m3fn).view(np.uint8)
    else:
        c = by_word.astype(ml_dtypes.float4_e2m1fn).view(np.uint8) & 0xF
        words = (c[..., 0::2] | (c[..., 1::2] << 4)).reshape(k // 512, 128, 2 * n)
    return np.ascontiguousarray(words), np.ascontiguousarray(byte.astype(np.uint8).reshape(k // 512, 16, n))


def unpack_weight(words, scales, fmt):
    g, _, n = scales.shape
    words = np.ascontiguousarray(words).reshape(g, 128, n, -1)
    if fmt == "e4m3":
        vals = words.view(ml_dtypes.float8_e4m3fn).astype(np.float64)
    else:
        nib = np.empty((g, 128, n, 4), np.uint8)
        nib[..., 0::2] = words & 0xF
        nib[..., 1::2] = words >> 4
        vals = E2M1[nib]
    vals = vals * np.repeat(np.exp2(scales.astype(np.float64) - 127.0), 8, axis=1)[..., None]
    return vals.transpose(0, 1, 3, 2).reshape(g * 512, n)


def gelu(v):
    return 0.5 * v * (1.0 + np.tanh(np.sqrt(2.0 / np.pi) * (v + 0.044715 * v**3)))


K, T, E, C, H, N = 512, 1024, 8, 256, 512, 256


def by_expert(wq, xq):
    return np.concatenate([wq[e].T @ xq[:, e * C:(e + 1) * C] for e in range(E)], axis=1)


def setup_inputs():
    n = np.random.standard_normal
    s = mx_kscale(K)[:, None]
    u = mx_kscale(H)
    first = np.random.permutation(np.repeat(np.arange(E), T // E))
    second = (first + 1 + np.random.permutation(np.repeat(np.arange(E - 1), -(-T // (E - 1)))[:T])) % E
    while np.bincount(second, minlength=E).max() != T // E:
        load = np.bincount(second, minlength=E); hi, lo = int(load.argmax()), int(load.argmin())
        t = np.flatnonzero((second == hi) & (first != lo))[0]; second[t] = lo
    slot_token = np.empty(E * C, np.int64); pos = np.empty((2, T), np.int64); fill = np.zeros(E, np.int64)
    place = np.stack([np.random.permutation(C) for _ in range(E)])
    for r, deal in enumerate((first, second)):
        for t in np.random.permutation(T):
            e = deal[t]; j = e * C + place[e, fill[e]]; fill[e] += 1; slot_token[j] = t; pos[r, t] = j
    g = np.random.uniform(0.2, 0.8, T)
    w1 = [pack_weight(m, "e2m1") for m in n((E, K, H)) / np.sqrt(K) / s[None] * u[None, None, :]]
    w2 = [pack_weight(m, "e2m1") for m in n((E, H, N)) / np.sqrt(H) / u[None, :, None]]
    return {
        "xT": (n((K, T)) * s).astype(np.float32),
        "w1_words": np.stack([m[0] for m in w1]),
        "w1_scales": np.stack([m[1] for m in w1]),
        "w2_words": np.stack([m[0] for m in w2]),
        "w2_scales": np.stack([m[1] for m in w2]),
        "gate": np.stack([np.tile(g, (N, 1)), np.tile(1.0 - g, (N, 1))]).astype(np.float32),
        "offs": striped(slot_token),
        "pos1": striped(pos[0]),
        "pos2": striped(pos[1]),
    }


def reference(xT, w1_words, w1_scales, w2_words, w2_scales, gate, offs, pos1, pos2):
    idx = unstriped(offs)
    w1 = np.stack([unpack_weight(w1_words[e], w1_scales[e], "e2m1") for e in range(E)])
    w2 = np.stack([unpack_weight(w2_words[e], w2_scales[e], "e2m1") for e in range(E)])
    xq = mxq(f64(xT)[:, idx], 0, "e4m3")
    h = gelu(by_expert(w1, xq))
    y = by_expert(w2, mxq(h, 0, "e4m3"))
    return f64(gate[0]) * y[:, unstriped(pos1)] + f64(gate[1]) * y[:, unstriped(pos2)]

@@ -1,0 +1,252 @@
+from contextlib import ExitStack
+
+import concourse.mybir as mybir
+from concourse.masks import make_identity
+
+K, T, E, C, H, N = 512, 1024, 8, 256, 512, 256
+S = E * C
+P = 128
+PACK = 4
+FLOPS = 2 * S * (K * H + H * N)
+
+F32 = mybir.dt.float32
+BF16 = mybir.dt.bfloat16
+I32 = mybir.dt.int32
+U32 = mybir.dt.uint32
+U16 = mybir.dt.uint16
+U8 = mybir.dt.uint8
+FP8X4 = mybir.dt.float8_e4m3fn_x4
+FP4X4 = mybir.dt.float4_e2m1fn_x4
+ACT = mybir.ActivationFunctionType
+ALU = mybir.AluOpType
+
+X_CHUNK = 256
+W1_EARLY = 4
+
+
+def tile_moe_pln_mlp_gelu_kernel(
+    tc, xT, w1_words, w1_scales, w2_words, w2_scales, gate, offs, pos1, pos2, out
+):
+    nc = tc.nc
+    with ExitStack() as ctx:
+        keep = ctx.enter_context(tc.tile_pool(name="keep", bufs=1))
+        psum = ctx.enter_context(tc.psum_pool(name="psum", bufs=1))
+
+        offs_sb = keep.tile([P, S // 16], U16, name="offs_sb")
+        pos_sb = [keep.tile([P, T // 16], U16, name="pos1_sb"), keep.tile([P, T // 16], U16, name="pos2_sb")]
+        s1_raw = keep.tile([P, H], U8, name="s1_raw", align_bytes=64)
+        s1_perm = keep.tile([P, H], U8, name="s1_perm", align_bytes=64)
+        s1 = keep.tile([P, E * H], U8, name="s1", align_bytes=64)
+        s2 = keep.tile([P, E * N], U8, name="s2", align_bytes=64)
+        w1_raw = keep.tile([P, E, 2 * H], U8, name="w1_raw", align_bytes=64)
+        w1 = keep.tile([P, E, 2 * H], U8, name="w1", align_bytes=64)
+        w2 = keep.tile([P, E, 2 * N], U8, name="w2", align_bytes=64)
+        x_raw = [keep.tile([P, PACK, X_CHUNK], F32, name="x_raw%d" % c) for c in range(T // X_CHUNK)]
+        x_bf = keep.tile([P, T * PACK], BF16, name="x_bf", align_bytes=64)
+        x_codes = keep.tile([P, T], U32, name="x_codes", align_bytes=64)
+        x_scales = keep.tile([P, T], U8, name="x_scales", align_bytes=64)
+        slot_codes = keep.tile([P, S], U32, name="slot_codes", align_bytes=64)
+        slot_scales = keep.tile([P, S], U8, name="slot_scales", align_bytes=64)
+        h_bf = keep.tile([P, S * PACK], BF16, name="h_bf", align_bytes=64)
+        h_codes = keep.tile([P, S], U32, name="h_codes", align_bytes=64)
+        h_scales = keep.tile([P, S], U8, name="h_scales", align_bytes=64)
+        y = [keep.tile([P, S], F32, name="y%d" % half) for half in range(2)]
+        gate_sb = [keep.tile([P, 2, T], F32, name="gate%d" % half) for half in range(2)]
+        picked = [keep.tile([P, 2, T], F32, name="picked%d" % half) for half in range(2)]
+        result = [keep.tile([P, T], F32, name="result%d" % half) for half in range(2)]
+        turned = keep.tile([P, 2 * T], F32, name="turned")
+        ident = keep.tile([P, P], F32, name="ident")
+        warm = keep.tile([P, 16], F32, name="warm")
+
+        nc.vector.memset(warm[:, 0:8], 0.0)
+        nc.scalar.activation(warm[:, 8:16], warm[:, 0:8], ACT.Gelu_apprx_tanh)
+        nc.gpsimd.memset(x_scales[:], 0)
+        make_identity(nc, ident[:])
+        nc.vector.memset(s1[:].bitcast(I32), 0)
+        nc.vector.memset(s2[:].bitcast(I32), 0)
+
+        w1_hbm = w1_words.rearrange("e s p b -> p (e s) b").bitcast(I32)
+        x_hbm = xT.rearrange("(p j) t -> p j t", j=PACK)
+
+        nc.sync.dma_start(s1_raw[:].bitcast(I32), w1_scales.rearrange("e s q i -> q (e s) i").bitcast(I32))
+        nc.sync.dma_start(w1_raw[:, 0:W1_EARLY, :].bitcast(I32), w1_hbm[:, 0:W1_EARLY, :])
+        for c in range(T // X_CHUNK):
+            nc.sync.dma_start(x_raw[c][:], x_hbm[:, :, c * X_CHUNK : (c + 1) * X_CHUNK])
+        nc.sync.dma_start(offs_sb[:], offs)
+
+        nc.vector.tensor_copy(
+            s1_perm[:].rearrange("p (d m) -> p d m", d=PACK), s1_raw[:].rearrange("p (m d) -> p d m", d=PACK)
+        )
+        for quad in range(4):
+            nc.sync.dma_start(
+                s1[32 * quad : 32 * quad + 4, :].bitcast(I32), s1_perm[32 * quad : 32 * quad + 32, :].bitcast(I32)
+            )
+        nc.sync.dma_start(w1_raw[:, W1_EARLY:E, :].bitcast(I32), w1_hbm[:, W1_EARLY:E, :])
+        s2_hbm = w2_scales.rearrange("e s q n -> q (e s) n").bitcast(I32)
+        for quad in range(4):
+            nc.sync.dma_start(
+                s2[32 * quad : 32 * quad + 4, :].bitcast(I32).rearrange("p (e n) -> p e n", e=E),
+                s2_hbm[4 * quad : 4 * quad + 4],
+            )
+        nc.sync.dma_start(w2[:].bitcast(I32), w2_words.rearrange("e s p b -> p (e s) b").bitcast(I32))
+        nc.sync.dma_start(pos_sb[0][:], pos1)
+        nc.sync.dma_start(pos_sb[1][:], pos2)
+        gate_hbm = gate.rearrange("r (h p) t -> p h r t", p=P)
+        for half in range(2):
+            nc.sync.dma_start(gate_sb[half][:], gate_hbm[:, half])
+
+        def permute_w1(e0, e1):
+            nc.vector.tensor_copy(
+                w1[:, e0:e1, :].bitcast(U16).rearrange("p e (d m) -> p e d m", d=PACK),
+                w1_raw[:, e0:e1, :].bitcast(U16).rearrange("p e (m d) -> p e d m", d=PACK),
+            )
+
+        def x_views(c, t0, t1):
+            first = c * X_CHUNK
+            dst = x_bf[:, (first + t0) * PACK : (first + t1) * PACK].rearrange("p (c i j) -> p c j i", i=4, j=PACK)
+            src = x_raw[c][:, :, t0:t1].rearrange("p j (c i) -> p c j i", i=4)
+            return dst, src
+
+        def quantize_x(c):
+            cols = slice(c * X_CHUNK, (c + 1) * X_CHUNK)
+            nc.vector.quantize_mx(
+                out=x_codes[:, cols].bitcast(FP8X4),
+                scales=x_scales[:, cols],
+                in_=x_bf[:, c * X_CHUNK * PACK : (c + 1) * X_CHUNK * PACK],
+            )
+
+        permute_w1(0, 2)
+        permute_w1(2, 4)
+        scalar_share = [192, 192, 160, 96]
+        for c in range(T // X_CHUNK):
+            dst, src = x_views(c, 0, scalar_share[c])
+            nc.scalar.activation(dst, src, ACT.Copy)
+            dst, src = x_views(c, scalar_share[c], X_CHUNK)
+            nc.vector.tensor_copy(dst, src)
+            if c > 0:
+                quantize_x(c - 1)
+        quantize_x(T // X_CHUNK - 1)
+
+        def gather_slots(j0, j1):
+            offsets = offs_sb[:, j0 // 16 : j1 // 16]
+            nc.vector.tensor_copy(slot_codes[:, j0:j1], x_codes[:].indirect(offsets))
+            nc.vector.tensor_copy(slot_scales[:, j0:j1], x_scales[:].indirect(offsets))
+
+        def first_layer(j0):
+            e = j0 // C
+            block = j0 // P
+            bank = psum.tile([P, PACK, P], F32, name="a_bank%d" % (block % 5))
+            for d in range(PACK):
+                nc.tensor.matmul_mx(
+                    out=bank[:, d, :],
+                    lhsT=w1[:, e, 2 * P * d : 2 * P * (d + 1)].bitcast(FP4X4),
+                    lhsT_scale=s1[:, e * H + P * d : e * H + P * (d + 1)],
+                    rhs=slot_codes[:, j0 : j0 + P].bitcast(FP8X4),
+                    rhs_scale=slot_scales[:, j0 : j0 + P],
+                    start=True,
+                    stop=True,
+                )
+            nc.scalar.activation(
+                h_bf[:, j0 * PACK : (j0 + P) * PACK].rearrange("p (c d) -> p c d", d=PACK),
+                bank[:].rearrange("p d c -> p c d"),
+                ACT.Gelu_apprx_tanh,
+            )
+
+        def quantize_h(j0, j1):
+            nc.vector.quantize_mx(
+                out=h_codes[:, j0:j1].bitcast(FP8X4), scales=h_scales[:, j0:j1], in_=h_bf[:, j0 * PACK : j1 * PACK]
+            )
+
+        def second_layer(half, j0, j1, tag, on_vector=False):
+            bank = psum.tile([P, 2 * C], F32, name="y_bank%d" % tag)
+            step = min(C, j1 - j0)
+            for j in range(j0, j1, step):
+                e = j // C
+                nc.tensor.matmul_mx(
+                    out=bank[:, j - j0 : j - j0 + step],
+                    lhsT=w2[:, e, 2 * P * half : 2 * P * (half + 1)].bitcast(FP4X4),
+                    lhsT_scale=s2[:, e * N + P * half : e * N + P * (half + 1)],
+                    rhs=h_codes[:, j : j + step].bitcast(FP8X4),
+                    rhs_scale=h_scales[:, j : j + step],
+                    start=True,
+                    stop=True,
+                )
+            if on_vector:
+                nc.vector.tensor_copy(y[half][:, j0:j1], bank[:, 0 : j1 - j0])
+            else:
+                nc.scalar.activation(y[half][:, j0:j1], bank[:, 0 : j1 - j0], ACT.Copy)
+
+        lag = 4
+        for e in range(E):
+            if e in (3, 5):
+                permute_w1(e + 1, e + 3)
+            if e < E - 1:
+                gather_slots(e * C, (e + 1) * C)
+                first_layer(e * C)
+                first_layer(e * C + P)
+            else:
+                for j0 in (e * C, e * C + P):
+                    gather_slots(j0, j0 + P)
+                    first_layer(j0)
+            if e in (4, 6):
+                quantize_h((e - lag) * C, (e - lag + 2) * C)
+                second_layer(0, (e - lag) * C, (e - lag + 2) * C, (e // 2) % 3)
+        quantize_h(4 * C, 6 * C)
+        second_layer(0, 4 * C, 6 * C, 1)
+        quantize_h(6 * C, 7 * C)
+        second_layer(0, 6 * C, 7 * C, 2)
+        quantize_h(7 * C, 7 * C + P)
+        second_layer(0, 7 * C, 7 * C + P, 0)
+        quantize_h(7 * C + P, S)
+        second_layer(0, 7 * C + P, S, 1, on_vector=True)
+        for pair in range(E // 2):
+            second_layer(1, 2 * pair * C, (2 * pair + 2) * C, (pair + 2) % 3)
+
+        def pick(half, r, t0, t1):
+            nc.vector.tensor_tensor(
+                picked[half][:, r, t0:t1],
+                y[half][:].indirect(pos_sb[r][:, t0 // 16 : t1 // 16]),
+                gate_sb[half][:, r, t0:t1],
+                ALU.mult,
+            )
+
+        def store(half, t0, t1):
+            nc.sync.dma_start(out[half * P : (half + 1) * P, t0:t1], result[half][:, t0:t1])
+
+        def add_on_vector(half, t0, t1):
+            nc.vector.tensor_tensor(
+                result[half][:, t0:t1], picked[half][:, 0, t0:t1], picked[half][:, 1, t0:t1], ALU.add
+            )
+            store(half, t0, t1)
+
+        def add_on_tensor(n, half, t0, t1):
+            width = t1 - t0
+            sums = psum.tile([P, PACK * P], F32, name="a_bank%d" % (2 * n % 5))
+            for b in range(0, width, P):
+                for r in range(2):
+                    nc.tensor.matmul(
+                        sums[:, b : b + P],
+                        lhsT=picked[half][:, r, t0 + b : t0 + b + P],
+                        rhs=ident[:],
+                        start=(r == 0),
+                        stop=(r == 1),
+                        is_transpose=True,
+                    )
+            cols = slice(half * T + t0, half * T + t1)
+            nc.scalar.activation(turned[:, cols], sums[:, 0:width], ACT.Copy)
+            back = psum.tile([P, PACK * P], F32, name="a_bank%d" % ((2 * n + 1) % 5))
+            for b in range(0, width, P):
+                nc.tensor.transpose(back[:, b : b + P], turned[:, cols.start + b : cols.start + b + P], ident[:])
+            nc.scalar.activation(result[half][:, t0:t1], back[:, 0:width], ACT.Copy)
+            store(half, t0, t1)
+
+        for n, piece in enumerate([(0, 0, 512), (0, 512, 1024), (1, 0, 256), (1, 256, 512)]):
+            pick(piece[0], 0, piece[1], piece[2])
+            pick(piece[0], 1, piece[1], piece[2])
+            add_on_tensor(n, *piece)
+        pick(1, 0, 512, 896)
+        pick(1, 1, 512, 896)
+        pick(1, 0, 896, T)
+        add_on_vector(1, 512, 896)
+        pick(1, 1, 896, T)
+        add_on_vector(1, 896, T)

@@ -20,7 +20,7 @@ FP4X4 = mybir.dt.float4_e2m1fn_x4
 ACT = mybir.ActivationFunctionType
 ALU = mybir.AluOpType
 
-X_CHUNK = 256
+X_CHUNKS = [(0, 512), (512, 768), (768, 1024)]
 W1_EARLY = 4
 
 
@@ -34,14 +34,11 @@ def tile_moe_pln_mlp_gelu_kernel(
 
         offs_sb = keep.tile([P, S // 16], U16, name="offs_sb")
         pos_sb = [keep.tile([P, T // 16], U16, name="pos1_sb"), keep.tile([P, T // 16], U16, name="pos2_sb")]
-        s1_raw = keep.tile([P, H], U8, name="s1_raw", align_bytes=64)
+        s1_raw = keep.tile([P, H], U8, name="s1_raw", tag="after_s1", align_bytes=64)
         s1_perm = keep.tile([P, H], U8, name="s1_perm", align_bytes=64)
         s1 = keep.tile([P, E * H], U8, name="s1", align_bytes=64)
-        s2 = keep.tile([P, E * N], U8, name="s2", align_bytes=64)
-        w1_raw = keep.tile([P, E, 2 * H], U8, name="w1_raw", align_bytes=64)
         w1 = keep.tile([P, E, 2 * H], U8, name="w1", align_bytes=64)
-        w2 = keep.tile([P, E, 2 * N], U8, name="w2", align_bytes=64)
-        x_raw = [keep.tile([P, PACK, X_CHUNK], F32, name="x_raw%d" % c) for c in range(T // X_CHUNK)]
+        x_raw = [keep.tile([P, PACK, t1 - t0], F32, name="x_raw", tag="after_x%d" % t0, align_bytes=64) for t0, t1 in X_CHUNKS]
         x_bf = keep.tile([P, T * PACK], BF16, name="x_bf", align_bytes=64)
         x_codes = keep.tile([P, T], U32, name="x_codes", align_bytes=64)
         x_scales = keep.tile([P, T], U8, name="x_scales", align_bytes=64)
@@ -51,7 +48,6 @@ def tile_moe_pln_mlp_gelu_kernel(
         h_codes = keep.tile([P, S], U32, name="h_codes", align_bytes=64)
         h_scales = keep.tile([P, S], U8, name="h_scales", align_bytes=64)
         y = [keep.tile([P, S], F32, name="y%d" % half) for half in range(2)]
-        gate_sb = [keep.tile([P, 2, T], F32, name="gate%d" % half) for half in range(2)]
         picked = [keep.tile([P, 2, T], F32, name="picked%d" % half) for half in range(2)]
         result = [keep.tile([P, T], F32, name="result%d" % half) for half in range(2)]
         turned = keep.tile([P, 2 * T], F32, name="turned")
@@ -63,69 +59,79 @@ def tile_moe_pln_mlp_gelu_kernel(
         nc.gpsimd.memset(x_scales[:], 0)
         make_identity(nc, ident[:])
         nc.vector.memset(s1[:].bitcast(I32), 0)
-        nc.vector.memset(s2[:].bitcast(I32), 0)
 
         w1_hbm = w1_words.rearrange("e s p b -> p (e s) b").bitcast(I32)
         x_hbm = xT.rearrange("(p j) t -> p j t", j=PACK)
 
+        def load_w1(e0):
+            raw = keep.tile([P, W1_EARLY, 2 * H], U8, name="w1_raw", align_bytes=64)
+            nc.sync.dma_start(raw[:].bitcast(I32), w1_hbm[:, e0 : e0 + W1_EARLY, :])
+            return raw
+
+        def permute_w1(raw, e0, e1):
+            nc.vector.tensor_copy(
+                w1[:, e0:e1, :].bitcast(U16).rearrange("p e (d m) -> p e d m", d=PACK),
+                raw[:, e0 % W1_EARLY : (e1 - 1) % W1_EARLY + 1, :].bitcast(U16).rearrange("p e (m d) -> p e d m", d=PACK),
+            )
+
         nc.sync.dma_start(s1_raw[:].bitcast(I32), w1_scales.rearrange("e s q i -> q (e s) i").bitcast(I32))
-        nc.sync.dma_start(w1_raw[:, 0:W1_EARLY, :].bitcast(I32), w1_hbm[:, 0:W1_EARLY, :])
-        for c in range(T // X_CHUNK):
-            nc.sync.dma_start(x_raw[c][:], x_hbm[:, :, c * X_CHUNK : (c + 1) * X_CHUNK])
+        w1_first = load_w1(0)
+        for c, (t0, t1) in enumerate(X_CHUNKS):
+            nc.sync.dma_start(x_raw[c][:], x_hbm[:, :, t0:t1])
         nc.sync.dma_start(offs_sb[:], offs)
+        nc.sync.dma_start(pos_sb[0][:], pos1)
+        nc.sync.dma_start(pos_sb[1][:], pos2)
 
         nc.vector.tensor_copy(
             s1_perm[:].rearrange("p (d m) -> p d m", d=PACK), s1_raw[:].rearrange("p (m d) -> p d m", d=PACK)
         )
-        for quad in range(4):
+        for quad in (0, 2, 1, 3):
             nc.sync.dma_start(
                 s1[32 * quad : 32 * quad + 4, :].bitcast(I32), s1_perm[32 * quad : 32 * quad + 32, :].bitcast(I32)
             )
-        nc.sync.dma_start(w1_raw[:, W1_EARLY:E, :].bitcast(I32), w1_hbm[:, W1_EARLY:E, :])
+        permute_w1(w1_first, 0, 2)
+        permute_w1(w1_first, 2, 4)
+        w1_second = load_w1(W1_EARLY)
+        s2 = keep.tile([P, E * N], U8, name="s2", tag="after_s1", align_bytes=64)
+        nc.vector.memset(s2[:].bitcast(I32), 0)
         s2_hbm = w2_scales.rearrange("e s q n -> q (e s) n").bitcast(I32)
-        for quad in range(4):
+        for quad in (0, 2, 1, 3):
             nc.sync.dma_start(
                 s2[32 * quad : 32 * quad + 4, :].bitcast(I32).rearrange("p (e n) -> p e n", e=E),
                 s2_hbm[4 * quad : 4 * quad + 4],
             )
-        nc.sync.dma_start(w2[:].bitcast(I32), w2_words.rearrange("e s p b -> p (e s) b").bitcast(I32))
-        nc.sync.dma_start(pos_sb[0][:], pos1)
-        nc.sync.dma_start(pos_sb[1][:], pos2)
-        gate_hbm = gate.rearrange("r (h p) t -> p h r t", p=P)
-        for half in range(2):
-            nc.sync.dma_start(gate_sb[half][:], gate_hbm[:, half])
-
-        def permute_w1(e0, e1):
-            nc.vector.tensor_copy(
-                w1[:, e0:e1, :].bitcast(U16).rearrange("p e (d m) -> p e d m", d=PACK),
-                w1_raw[:, e0:e1, :].bitcast(U16).rearrange("p e (m d) -> p e d m", d=PACK),
-            )
 
         def x_views(c, t0, t1):
-            first = c * X_CHUNK
+            first = X_CHUNKS[c][0]
             dst = x_bf[:, (first + t0) * PACK : (first + t1) * PACK].rearrange("p (c i j) -> p c j i", i=4, j=PACK)
             src = x_raw[c][:, :, t0:t1].rearrange("p j (c i) -> p c j i", i=4)
             return dst, src
 
-        def quantize_x(c):
-            cols = slice(c * X_CHUNK, (c + 1) * X_CHUNK)
+        def quantize_x(t0, t1):
             nc.vector.quantize_mx(
-                out=x_codes[:, cols].bitcast(FP8X4),
-                scales=x_scales[:, cols],
-                in_=x_bf[:, c * X_CHUNK * PACK : (c + 1) * X_CHUNK * PACK],
+                out=x_codes[:, t0:t1].bitcast(FP8X4), scales=x_scales[:, t0:t1], in_=x_bf[:, t0 * PACK : t1 * PACK]
             )
 
-        permute_w1(0, 2)
-        permute_w1(2, 4)
-        scalar_share = [192, 192, 160, 96]
-        for c in range(T // X_CHUNK):
+        scalar_share = [256, 192, 96]
+        for c, (t0, t1) in enumerate(X_CHUNKS):
             dst, src = x_views(c, 0, scalar_share[c])
             nc.scalar.activation(dst, src, ACT.Copy)
-            dst, src = x_views(c, scalar_share[c], X_CHUNK)
+            dst, src = x_views(c, scalar_share[c], t1 - t0)
             nc.vector.tensor_copy(dst, src)
-            if c > 0:
-                quantize_x(c - 1)
-        quantize_x(T // X_CHUNK - 1)
+            if c == 0:
+                quantize_x(256, 512)
+                quantize_x(0, 256)
+        quantize_x(512, 768)
+        quantize_x(768, 1024)
+
+        w2 = keep.tile([P, E, 2 * N], U8, name="w2", tag="after_x0", align_bytes=64)
+        nc.sync.dma_start(w2[:].bitcast(I32), w2_words.rearrange("e s p b -> p (e s) b").bitcast(I32))
+        gate_hbm = gate.rearrange("r (h p) t -> p h r t", p=P)
+        gate_sb = []
+        for half in range(2):
+            tile = keep.tile([P, 2, T], F32, name="gate_sb", tag="after_x%d" % X_CHUNKS[half + 1][0], align_bytes=64)
+            nc.sync.dma_start(tile[:], gate_hbm[:, half])
+            gate_sb.append(tile)
 
         def gather_slots(j0, j1):
             offsets = offs_sb[:, j0 // 16 : j1 // 16]
@@ -158,7 +164,7 @@ def tile_moe_pln_mlp_gelu_kernel(
             )
 
         def second_layer(half, j0, j1, tag, on_vector=False):
-            bank = psum.tile([P, 2 * C], F32, name="y_bank%d" % tag)
+            bank = psum.tile([P, 2 * C], F32, name=tag)
             step = min(C, j1 - j0)
             for j in range(j0, j1, step):
                 e = j // C
@@ -176,10 +182,9 @@ def tile_moe_pln_mlp_gelu_kernel(
             else:
                 nc.scalar.activation(y[half][:, j0:j1], bank[:, 0 : j1 - j0], ACT.Copy)
 
-        lag = 4
         for e in range(E):
             if e in (3, 5):
-                permute_w1(e + 1, e + 3)
+                permute_w1(w1_second, e + 1, e + 3)
             if e < E - 1:
                 gather_slots(e * C, (e + 1) * C)
                 first_layer(e * C)
@@ -188,19 +193,21 @@ def tile_moe_pln_mlp_gelu_kernel(
                 for j0 in (e * C, e * C + P):
                     gather_slots(j0, j0 + P)
                     first_layer(j0)
-            if e in (4, 6):
-                quantize_h((e - lag) * C, (e - lag + 2) * C)
-                second_layer(0, (e - lag) * C, (e - lag + 2) * C, (e // 2) % 3)
+            if e == 4:
+                quantize_h(0, 2 * C)
+                second_layer(0, 0, 2 * C, "y_bank0")
+        quantize_h(2 * C, 4 * C)
+        second_layer(0, 2 * C, 4 * C, "y_bank1")
         quantize_h(4 * C, 6 * C)
-        second_layer(0, 4 * C, 6 * C, 1)
+        second_layer(0, 4 * C, 6 * C, "y_bank2")
         quantize_h(6 * C, 7 * C)
-        second_layer(0, 6 * C, 7 * C, 2)
+        second_layer(0, 6 * C, 7 * C, "y_bank0")
         quantize_h(7 * C, 7 * C + P)
-        second_layer(0, 7 * C, 7 * C + P, 0)
+        second_layer(0, 7 * C, 7 * C + P, "a_bank1", on_vector=True)
         quantize_h(7 * C + P, S)
-        second_layer(0, 7 * C + P, S, 1, on_vector=True)
+        second_layer(0, 7 * C + P, S, "a_bank2", on_vector=True)
         for pair in range(E // 2):
-            second_layer(1, 2 * pair * C, (2 * pair + 2) * C, (pair + 2) % 3)
+            second_layer(1, 2 * pair * C, (2 * pair + 2) * C, "y_bank%d" % ((pair + 1) % 3))
 
         def pick(half, r, t0, t1):
             nc.vector.tensor_tensor(

@@ -56,7 +56,7 @@ def tile_moe_pln_mlp_gelu_kernel(
 
         nc.vector.memset(warm[:, 0:8], 0.0)
         nc.scalar.activation(warm[:, 8:16], warm[:, 0:8], ACT.Gelu_apprx_tanh)
-        nc.gpsimd.memset(x_scales[:], 0)
+        nc.vector.memset(x_scales[:].bitcast(I32), 0)
         make_identity(nc, ident[:])
         nc.vector.memset(s1[:].bitcast(I32), 0)
 
@@ -64,18 +64,19 @@ def tile_moe_pln_mlp_gelu_kernel(
         x_hbm = xT.rearrange("(p j) t -> p j t", j=PACK)
 
         def load_w1(e0):
-            raw = keep.tile([P, W1_EARLY, 2 * H], U8, name="w1_raw", align_bytes=64)
+            raw = keep.tile([P, W1_EARLY, 2 * H], U8, name="w1_raw%d" % e0, align_bytes=64)
             nc.sync.dma_start(raw[:].bitcast(I32), w1_hbm[:, e0 : e0 + W1_EARLY, :])
             return raw
 
         def permute_w1(raw, e0, e1):
             nc.vector.tensor_copy(
-                w1[:, e0:e1, :].bitcast(U16).rearrange("p e (d m) -> p e d m", d=PACK),
-                raw[:, e0 % W1_EARLY : (e1 - 1) % W1_EARLY + 1, :].bitcast(U16).rearrange("p e (m d) -> p e d m", d=PACK),
+                w1[:, e0:e1, :].bitcast(U16).rearrange("p e (d g m) -> p e g d m", d=PACK, m=8),
+                raw[:, e0 % W1_EARLY : (e1 - 1) % W1_EARLY + 1, :].bitcast(U16).rearrange("p e (g m d) -> p e g d m", d=PACK, m=8),
             )
 
         nc.sync.dma_start(s1_raw[:].bitcast(I32), w1_scales.rearrange("e s q i -> q (e s) i").bitcast(I32))
         w1_first = load_w1(0)
+        w1_second = load_w1(W1_EARLY)
         for c, (t0, t1) in enumerate(X_CHUNKS):
             nc.sync.dma_start(x_raw[c][:], x_hbm[:, :, t0:t1])
         nc.sync.dma_start(offs_sb[:], offs)
@@ -91,7 +92,8 @@ def tile_moe_pln_mlp_gelu_kernel(
             )
         permute_w1(w1_first, 0, 2)
         permute_w1(w1_first, 2, 4)
-        w1_second = load_w1(W1_EARLY)
+        permute_w1(w1_second, 4, 6)
+        permute_w1(w1_second, 6, 8)
         s2 = keep.tile([P, E * N], U8, name="s2", tag="after_s1", align_bytes=64)
         nc.vector.memset(s2[:].bitcast(I32), 0)
         s2_hbm = w2_scales.rearrange("e s q n -> q (e s) n").bitcast(I32)
@@ -112,17 +114,26 @@ def tile_moe_pln_mlp_gelu_kernel(
                 out=x_codes[:, t0:t1].bitcast(FP8X4), scales=x_scales[:, t0:t1], in_=x_bf[:, t0 * PACK : t1 * PACK]
             )
 
-        scalar_share = [256, 192, 96]
-        for c, (t0, t1) in enumerate(X_CHUNKS):
-            dst, src = x_views(c, 0, scalar_share[c])
+        def cast_on_scalar(c, t0, t1):
+            dst, src = x_views(c, t0, t1)
             nc.scalar.activation(dst, src, ACT.Copy)
-            dst, src = x_views(c, scalar_share[c], t1 - t0)
+
+        def cast_on_vector(c, t0, t1):
+            dst, src = x_views(c, t0, t1)
             nc.vector.tensor_copy(dst, src)
-            if c == 0:
-                quantize_x(256, 512)
-                quantize_x(0, 256)
+
+        cast_on_scalar(0, 0, 256)
+        cast_on_vector(0, 256, 512)
+        quantize_x(256, 512)
+        quantize_x(0, 256)
+        cast_on_scalar(1, 0, 160)
+        cast_on_vector(1, 160, 256)
         quantize_x(512, 768)
-        quantize_x(768, 1024)
+        cast_on_scalar(2, 0, 80)
+        cast_on_vector(2, 128, 256)
+        cast_on_vector(2, 80, 128)
+        quantize_x(896, 1024)
+        quantize_x(768, 896)
 
         w2 = keep.tile([P, E, 2 * N], U8, name="w2", tag="after_x0", align_bytes=64)
         nc.sync.dma_start(w2[:].bitcast(I32), w2_words.rearrange("e s p b -> p (e s) b").bitcast(I32))
@@ -141,7 +152,7 @@ def tile_moe_pln_mlp_gelu_kernel(
         def first_layer(j0):
             e = j0 // C
             block = j0 // P
-            bank = psum.tile([P, PACK, P], F32, name="a_bank%d" % (block % 5))
+            bank = psum.tile([P, PACK, P], F32, name="bank%d" % (block % 8))
             for d in range(PACK):
                 nc.tensor.matmul_mx(
                     out=bank[:, d, :],
@@ -163,9 +174,8 @@ def tile_moe_pln_mlp_gelu_kernel(
                 out=h_codes[:, j0:j1].bitcast(FP8X4), scales=h_scales[:, j0:j1], in_=h_bf[:, j0 * PACK : j1 * PACK]
             )
 
-        def second_layer(half, j0, j1, tag, on_vector=False):
+        def second_layer(half, j0, j1, tag, step=C, on_vector=False):
             bank = psum.tile([P, 2 * C], F32, name=tag)
-            step = min(C, j1 - j0)
             for j in range(j0, j1, step):
                 e = j // C
                 nc.tensor.matmul_mx(
@@ -183,31 +193,21 @@ def tile_moe_pln_mlp_gelu_kernel(
                 nc.scalar.activation(y[half][:, j0:j1], bank[:, 0 : j1 - j0], ACT.Copy)
 
         for e in range(E):
-            if e in (3, 5):
-                permute_w1(w1_second, e + 1, e + 3)
-            if e < E - 1:
-                gather_slots(e * C, (e + 1) * C)
-                first_layer(e * C)
-                first_layer(e * C + P)
-            else:
-                for j0 in (e * C, e * C + P):
-                    gather_slots(j0, j0 + P)
-                    first_layer(j0)
-            if e == 4:
-                quantize_h(0, 2 * C)
-                second_layer(0, 0, 2 * C, "y_bank0")
+            gather_slots(e * C, (e + 1) * C)
+            first_layer(e * C)
+            first_layer(e * C + P)
+        quantize_h(0, 2 * C)
+        second_layer(0, 0, 2 * C, "bank0")
         quantize_h(2 * C, 4 * C)
-        second_layer(0, 2 * C, 4 * C, "y_bank1")
+        second_layer(0, 2 * C, 4 * C, "bank1")
         quantize_h(4 * C, 6 * C)
-        second_layer(0, 4 * C, 6 * C, "y_bank2")
+        second_layer(0, 4 * C, 6 * C, "bank2")
         quantize_h(6 * C, 7 * C)
-        second_layer(0, 6 * C, 7 * C, "y_bank0")
-        quantize_h(7 * C, 7 * C + P)
-        second_layer(0, 7 * C, 7 * C + P, "a_bank1", on_vector=True)
-        quantize_h(7 * C + P, S)
-        second_layer(0, 7 * C + P, S, "a_bank2", on_vector=True)
+        second_layer(0, 6 * C, 7 * C, "bank3", on_vector=True)
+        quantize_h(7 * C, S)
+        second_layer(0, 7 * C, S, "bank4", on_vector=True)
         for pair in range(E // 2):
-            second_layer(1, 2 * pair * C, (2 * pair + 2) * C, "y_bank%d" % ((pair + 1) % 3))
+            second_layer(1, 2 * pair * C, (2 * pair + 2) * C, "bank%d" % ((5 + pair) % 8))
 
         def pick(half, r, t0, t1):
             nc.vector.tensor_tensor(
@@ -224,11 +224,10 @@ def tile_moe_pln_mlp_gelu_kernel(
             nc.vector.tensor_tensor(
                 result[half][:, t0:t1], picked[half][:, 0, t0:t1], picked[half][:, 1, t0:t1], ALU.add
             )
-            store(half, t0, t1)
 
         def add_on_tensor(n, half, t0, t1):
             width = t1 - t0
-            sums = psum.tile([P, PACK * P], F32, name="a_bank%d" % (2 * n % 5))
+            sums = psum.tile([P, PACK * P], F32, name="bank%d" % (1 + n % 2))
             for b in range(0, width, P):
                 for r in range(2):
                     nc.tensor.matmul(
@@ -241,19 +240,24 @@ def tile_moe_pln_mlp_gelu_kernel(
                     )
             cols = slice(half * T + t0, half * T + t1)
             nc.scalar.activation(turned[:, cols], sums[:, 0:width], ACT.Copy)
-            back = psum.tile([P, PACK * P], F32, name="a_bank%d" % ((2 * n + 1) % 5))
+            back = psum.tile([P, PACK * P], F32, name="bank%d" % (3 + n % 2))
             for b in range(0, width, P):
                 nc.tensor.transpose(back[:, b : b + P], turned[:, cols.start + b : cols.start + b + P], ident[:])
             nc.scalar.activation(result[half][:, t0:t1], back[:, 0:width], ACT.Copy)
-            store(half, t0, t1)
 
-        for n, piece in enumerate([(0, 0, 512), (0, 512, 1024), (1, 0, 256), (1, 256, 512)]):
-            pick(piece[0], 0, piece[1], piece[2])
-            pick(piece[0], 1, piece[1], piece[2])
-            add_on_tensor(n, *piece)
-        pick(1, 0, 512, 896)
-        pick(1, 1, 512, 896)
+        for n, (half, t0) in enumerate([(0, 0), (0, 256), (1, 0), (1, 256), (0, 512), (0, 768)]):
+            pick(half, 0, t0, t0 + 256)
+            pick(half, 1, t0, t0 + 256)
+            add_on_tensor(n, half, t0, t0 + 256)
+            if n % 2 == 1:
+                store(half, t0 - 256, t0 + 256)
+        pick(1, 0, 512, 768)
+        pick(1, 1, 512, 768)
+        pick(1, 0, 768, 896)
+        add_on_vector(1, 512, 768)
+        pick(1, 1, 768, 896)
         pick(1, 0, 896, T)
-        add_on_vector(1, 512, 896)
+        add_on_vector(1, 768, 896)
         pick(1, 1, 896, T)
         add_on_vector(1, 896, T)
+        store(1, 512, T)

@@ -48,7 +48,6 @@ def tile_moe_pln_mlp_gelu_kernel(
         h_codes = keep.tile([P, S], U32, name="h_codes", align_bytes=64)
         h_scales = keep.tile([P, S], U8, name="h_scales", align_bytes=64)
         y = [keep.tile([P, S], F32, name="y%d" % half) for half in range(2)]
-        picked = [keep.tile([P, 2, T], F32, name="picked%d" % half) for half in range(2)]
         result = [keep.tile([P, T], F32, name="result%d" % half) for half in range(2)]
         turned = keep.tile([P, 2 * T], F32, name="turned")
         ident = keep.tile([P, P], F32, name="ident")
@@ -203,15 +202,18 @@ def tile_moe_pln_mlp_gelu_kernel(
         quantize_h(4 * C, 6 * C)
         second_layer(0, 4 * C, 6 * C, "bank2")
         quantize_h(6 * C, 7 * C)
-        second_layer(0, 6 * C, 7 * C, "bank3", on_vector=True)
+        second_layer(0, 6 * C, 7 * C, "bank3")
         quantize_h(7 * C, S)
         second_layer(0, 7 * C, S, "bank4", on_vector=True)
         for pair in range(E // 2):
             second_layer(1, 2 * pair * C, (2 * pair + 2) * C, "bank%d" % ((5 + pair) % 8))
 
-        def pick(half, r, t0, t1):
+        def new_piece():
+            return keep.tile([P, 2, 256], F32, name="picked", bufs=2)
+
+        def pick(picked, half, r, t0, t1):
             nc.vector.tensor_tensor(
-                picked[half][:, r, t0:t1],
+                picked[:, r, 0 : t1 - t0],
                 y[half][:].indirect(pos_sb[r][:, t0 // 16 : t1 // 16]),
                 gate_sb[half][:, r, t0:t1],
                 ALU.mult,
@@ -220,19 +222,17 @@ def tile_moe_pln_mlp_gelu_kernel(
         def store(half, t0, t1):
             nc.sync.dma_start(out[half * P : (half + 1) * P, t0:t1], result[half][:, t0:t1])
 
-        def add_on_vector(half, t0, t1):
-            nc.vector.tensor_tensor(
-                result[half][:, t0:t1], picked[half][:, 0, t0:t1], picked[half][:, 1, t0:t1], ALU.add
-            )
+        def add_on_vector(picked, half, t0, t1):
+            nc.vector.tensor_tensor(result[half][:, t0:t1], picked[:, 0, 0 : t1 - t0], picked[:, 1, 0 : t1 - t0], ALU.add)
 
-        def add_on_tensor(n, half, t0, t1):
+        def add_on_tensor(n, picked, half, t0, t1):
             width = t1 - t0
             sums = psum.tile([P, PACK * P], F32, name="bank%d" % (1 + n % 2))
             for b in range(0, width, P):
                 for r in range(2):
                     nc.tensor.matmul(
                         sums[:, b : b + P],
-                        lhsT=picked[half][:, r, t0 + b : t0 + b + P],
+                        lhsT=picked[:, r, b : b + P],
                         rhs=ident[:],
                         start=(r == 0),
                         stop=(r == 1),
@@ -246,18 +246,23 @@ def tile_moe_pln_mlp_gelu_kernel(
             nc.scalar.activation(result[half][:, t0:t1], back[:, 0:width], ACT.Copy)
 
         for n, (half, t0) in enumerate([(0, 0), (0, 256), (1, 0), (1, 256), (0, 512), (0, 768)]):
-            pick(half, 0, t0, t0 + 256)
-            pick(half, 1, t0, t0 + 256)
-            add_on_tensor(n, half, t0, t0 + 256)
+            piece = new_piece()
+            pick(piece, half, 0, t0, t0 + 256)
+            pick(piece, half, 1, t0, t0 + 256)
+            add_on_tensor(n, piece, half, t0, t0 + 256)
             if n % 2 == 1:
                 store(half, t0 - 256, t0 + 256)
-        pick(1, 0, 512, 768)
-        pick(1, 1, 512, 768)
-        pick(1, 0, 768, 896)
-        add_on_vector(1, 512, 768)
-        pick(1, 1, 768, 896)
-        pick(1, 0, 896, T)
-        add_on_vector(1, 768, 896)
-        pick(1, 1, 896, T)
-        add_on_vector(1, 896, T)
+        waiting = None
+        for t0, t1 in [(512, 768), (768, 896), (896, T)]:
+            if waiting is None:
+                piece = new_piece()
+                pick(piece, 1, 0, t0, t1)
+            else:
+                last = piece
+                piece = new_piece()
+                pick(piece, 1, 0, t0, t1)
+                add_on_vector(last, 1, *waiting)
+            pick(piece, 1, 1, t0, t1)
+            waiting = (t0, t1)
+        add_on_vector(piece, 1, *waiting)
         store(1, 512, T)

@@ -7,6 +7,7 @@ K, T, E, C, H, N = 512, 1024, 8, 256, 512, 256
 S = E * C
 P = 128
 PACK = 4
+BANKS = 8
 FLOPS = 2 * S * (K * H + H * N)
 
 F32 = mybir.dt.float32
@@ -21,7 +22,11 @@ ACT = mybir.ActivationFunctionType
 ALU = mybir.AluOpType
 
 X_CHUNKS = [(0, 512), (512, 768), (768, 1024)]
-W1_EARLY = 4
+QUADRANTS = (0, 2, 1, 3)
+PIECE = 256
+TENSOR_PIECES = [(0, 0), (0, 256), (1, 0), (1, 256), (0, 512), (0, 768)]
+LONG_PIECE = (512, 896)
+SHORT_PIECE = (896, T)
 
 
 def tile_moe_pln_mlp_gelu_kernel(
@@ -38,7 +43,10 @@ def tile_moe_pln_mlp_gelu_kernel(
         s1_perm = keep.tile([P, H], U8, name="s1_perm", align_bytes=64)
         s1 = keep.tile([P, E * H], U8, name="s1", align_bytes=64)
         w1 = keep.tile([P, E, 2 * H], U8, name="w1", align_bytes=64)
-        x_raw = [keep.tile([P, PACK, t1 - t0], F32, name="x_raw", tag="after_x%d" % t0, align_bytes=64) for t0, t1 in X_CHUNKS]
+        x_raw = [
+            keep.tile([P, PACK, t1 - t0], F32, name="x_raw", tag="after_x%d" % t0, align_bytes=64)
+            for t0, t1 in X_CHUNKS
+        ]
         x_bf = keep.tile([P, T * PACK], BF16, name="x_bf", align_bytes=64)
         x_codes = keep.tile([P, T], U32, name="x_codes", align_bytes=64)
         x_scales = keep.tile([P, T], U8, name="x_scales", align_bytes=64)
@@ -62,20 +70,20 @@ def tile_moe_pln_mlp_gelu_kernel(
         w1_hbm = w1_words.rearrange("e s p b -> p (e s) b").bitcast(I32)
         x_hbm = xT.rearrange("(p j) t -> p j t", j=PACK)
 
-        def load_w1(e0):
-            raw = keep.tile([P, W1_EARLY, 2 * H], U8, name="w1_raw%d" % e0, align_bytes=64)
-            nc.sync.dma_start(raw[:].bitcast(I32), w1_hbm[:, e0 : e0 + W1_EARLY, :])
+        def load_w1(e0, e1):
+            raw = keep.tile([P, e1 - e0, 2 * H], U8, name="w1_raw%d" % e0, align_bytes=64)
+            nc.sync.dma_start(raw[:].bitcast(I32), w1_hbm[:, e0:e1, :])
             return raw
 
         def permute_w1(raw, e0, e1):
             nc.vector.tensor_copy(
                 w1[:, e0:e1, :].bitcast(U16).rearrange("p e (d g m) -> p e g d m", d=PACK, m=8),
-                raw[:, e0 % W1_EARLY : (e1 - 1) % W1_EARLY + 1, :].bitcast(U16).rearrange("p e (g m d) -> p e g d m", d=PACK, m=8),
+                raw[:, 0 : e1 - e0, :].bitcast(U16).rearrange("p e (g m d) -> p e g d m", d=PACK, m=8),
             )
 
         nc.sync.dma_start(s1_raw[:].bitcast(I32), w1_scales.rearrange("e s q i -> q (e s) i").bitcast(I32))
-        w1_first = load_w1(0)
-        w1_second = load_w1(W1_EARLY)
+        w1_first = load_w1(0, E // 2)
+        w1_second = load_w1(E // 2, E)
         for c, (t0, t1) in enumerate(X_CHUNKS):
             nc.sync.dma_start(x_raw[c][:], x_hbm[:, :, t0:t1])
         nc.sync.dma_start(offs_sb[:], offs)
@@ -85,41 +93,39 @@ def tile_moe_pln_mlp_gelu_kernel(
         nc.vector.tensor_copy(
             s1_perm[:].rearrange("p (d m) -> p d m", d=PACK), s1_raw[:].rearrange("p (m d) -> p d m", d=PACK)
         )
-        for quad in (0, 2, 1, 3):
+        for quad in QUADRANTS:
             nc.sync.dma_start(
                 s1[32 * quad : 32 * quad + 4, :].bitcast(I32), s1_perm[32 * quad : 32 * quad + 32, :].bitcast(I32)
             )
-        permute_w1(w1_first, 0, 2)
-        permute_w1(w1_first, 2, 4)
-        permute_w1(w1_second, 4, 6)
-        permute_w1(w1_second, 6, 8)
+        permute_w1(w1_first, 0, E // 2)
+        permute_w1(w1_second, E // 2, E)
         s2 = keep.tile([P, E * N], U8, name="s2", tag="after_s1", align_bytes=64)
         nc.vector.memset(s2[:].bitcast(I32), 0)
         s2_hbm = w2_scales.rearrange("e s q n -> q (e s) n").bitcast(I32)
-        for quad in (0, 2, 1, 3):
+        for quad in QUADRANTS:
             nc.sync.dma_start(
                 s2[32 * quad : 32 * quad + 4, :].bitcast(I32).rearrange("p (e n) -> p e n", e=E),
                 s2_hbm[4 * quad : 4 * quad + 4],
             )
 
-        def x_views(c, t0, t1):
+        def cast_views(c, t0, t1):
             first = X_CHUNKS[c][0]
             dst = x_bf[:, (first + t0) * PACK : (first + t1) * PACK].rearrange("p (c i j) -> p c j i", i=4, j=PACK)
             src = x_raw[c][:, :, t0:t1].rearrange("p j (c i) -> p c j i", i=4)
             return dst, src
 
+        def cast_on_scalar(c, t0, t1):
+            dst, src = cast_views(c, t0, t1)
+            nc.scalar.activation(dst, src, ACT.Copy)
+
+        def cast_on_vector(c, t0, t1):
+            dst, src = cast_views(c, t0, t1)
+            nc.vector.tensor_copy(dst, src)
+
         def quantize_x(t0, t1):
             nc.vector.quantize_mx(
                 out=x_codes[:, t0:t1].bitcast(FP8X4), scales=x_scales[:, t0:t1], in_=x_bf[:, t0 * PACK : t1 * PACK]
             )
-
-        def cast_on_scalar(c, t0, t1):
-            dst, src = x_views(c, t0, t1)
-            nc.scalar.activation(dst, src, ACT.Copy)
-
-        def cast_on_vector(c, t0, t1):
-            dst, src = x_views(c, t0, t1)
-            nc.vector.tensor_copy(dst, src)
 
         cast_on_scalar(0, 0, 256)
         cast_on_vector(0, 256, 512)
@@ -150,8 +156,7 @@ def tile_moe_pln_mlp_gelu_kernel(
 
         def first_layer(j0):
             e = j0 // C
-            block = j0 // P
-            bank = psum.tile([P, PACK, P], F32, name="bank%d" % (block % 8))
+            bank = psum.tile([P, PACK, P], F32, name="bank%d" % (j0 // P % BANKS))
             for d in range(PACK):
                 nc.tensor.matmul_mx(
                     out=bank[:, d, :],
@@ -168,48 +173,44 @@ def tile_moe_pln_mlp_gelu_kernel(
                 ACT.Gelu_apprx_tanh,
             )
 
-        def quantize_h(j0, j1):
+        def quantize_h(e0, e1):
+            j0, j1 = e0 * C, e1 * C
             nc.vector.quantize_mx(
                 out=h_codes[:, j0:j1].bitcast(FP8X4), scales=h_scales[:, j0:j1], in_=h_bf[:, j0 * PACK : j1 * PACK]
             )
 
-        def second_layer(half, j0, j1, tag, step=C, on_vector=False):
-            bank = psum.tile([P, 2 * C], F32, name=tag)
-            for j in range(j0, j1, step):
-                e = j // C
+        def second_layer(half, e0, e1, bank_number):
+            bank = psum.tile([P, 2 * C], F32, name="bank%d" % bank_number)
+            for e in range(e0, e1):
                 nc.tensor.matmul_mx(
-                    out=bank[:, j - j0 : j - j0 + step],
+                    out=bank[:, (e - e0) * C : (e - e0 + 1) * C],
                     lhsT=w2[:, e, 2 * P * half : 2 * P * (half + 1)].bitcast(FP4X4),
                     lhsT_scale=s2[:, e * N + P * half : e * N + P * (half + 1)],
-                    rhs=h_codes[:, j : j + step].bitcast(FP8X4),
-                    rhs_scale=h_scales[:, j : j + step],
+                    rhs=h_codes[:, e * C : (e + 1) * C].bitcast(FP8X4),
+                    rhs_scale=h_scales[:, e * C : (e + 1) * C],
                     start=True,
                     stop=True,
                 )
-            if on_vector:
-                nc.vector.tensor_copy(y[half][:, j0:j1], bank[:, 0 : j1 - j0])
-            else:
-                nc.scalar.activation(y[half][:, j0:j1], bank[:, 0 : j1 - j0], ACT.Copy)
+            return y[half][:, e0 * C : e1 * C], bank[:, 0 : (e1 - e0) * C]
 
         for e in range(E):
             gather_slots(e * C, (e + 1) * C)
             first_layer(e * C)
             first_layer(e * C + P)
-        quantize_h(0, 2 * C)
-        second_layer(0, 0, 2 * C, "bank0")
-        quantize_h(2 * C, 4 * C)
-        second_layer(0, 2 * C, 4 * C, "bank1")
-        quantize_h(4 * C, 6 * C)
-        second_layer(0, 4 * C, 6 * C, "bank2")
-        quantize_h(6 * C, 7 * C)
-        second_layer(0, 6 * C, 7 * C, "bank3")
-        quantize_h(7 * C, S)
-        second_layer(0, 7 * C, S, "bank4", on_vector=True)
+
+        for bank_number, (e0, e1) in enumerate([(0, 2), (2, 4), (4, 6), (6, 7)]):
+            quantize_h(e0, e1)
+            dst, src = second_layer(0, e0, e1, bank_number)
+            nc.scalar.activation(dst, src, ACT.Copy)
+        quantize_h(E - 1, E)
+        dst, src = second_layer(0, E - 1, E, 4)
+        nc.vector.tensor_copy(dst, src)
         for pair in range(E // 2):
-            second_layer(1, 2 * pair * C, (2 * pair + 2) * C, "bank%d" % ((5 + pair) % 8))
+            dst, src = second_layer(1, 2 * pair, 2 * pair + 2, (5 + pair) % BANKS)
+            nc.scalar.activation(dst, src, ACT.Copy)
 
         def new_piece():
-            return keep.tile([P, 2, 256], F32, name="picked", bufs=2)
+            return keep.tile([P, 2, LONG_PIECE[1] - LONG_PIECE[0]], F32, name="picked", bufs=2)
 
         def pick(picked, half, r, t0, t1):
             nc.vector.tensor_tensor(
@@ -219,16 +220,15 @@ def tile_moe_pln_mlp_gelu_kernel(
                 ALU.mult,
             )
 
-        def store(half, t0, t1):
-            nc.sync.dma_start(out[half * P : (half + 1) * P, t0:t1], result[half][:, t0:t1])
+        def store(queue, half, t0, t1):
+            queue.dma_start(out[half * P : (half + 1) * P, t0:t1], result[half][:, t0:t1])
 
-        def add_on_vector(picked, half, t0, t1):
-            nc.vector.tensor_tensor(result[half][:, t0:t1], picked[:, 0, 0 : t1 - t0], picked[:, 1, 0 : t1 - t0], ALU.add)
+        def add_on_vector(picked, t0, t1):
+            nc.vector.tensor_tensor(result[1][:, t0:t1], picked[:, 0, 0 : t1 - t0], picked[:, 1, 0 : t1 - t0], ALU.add)
 
-        def add_on_tensor(n, picked, half, t0, t1):
-            width = t1 - t0
+        def add_on_tensor(n, picked, half, t0):
             sums = psum.tile([P, PACK * P], F32, name="bank%d" % (1 + n % 2))
-            for b in range(0, width, P):
+            for b in range(0, PIECE, P):
                 for r in range(2):
                     nc.tensor.matmul(
                         sums[:, b : b + P],
@@ -238,31 +238,27 @@ def tile_moe_pln_mlp_gelu_kernel(
                         stop=(r == 1),
                         is_transpose=True,
                     )
-            cols = slice(half * T + t0, half * T + t1)
-            nc.scalar.activation(turned[:, cols], sums[:, 0:width], ACT.Copy)
+            first = half * T + t0
+            nc.scalar.activation(turned[:, first : first + PIECE], sums[:, 0:PIECE], ACT.Copy)
             back = psum.tile([P, PACK * P], F32, name="bank%d" % (3 + n % 2))
-            for b in range(0, width, P):
-                nc.tensor.transpose(back[:, b : b + P], turned[:, cols.start + b : cols.start + b + P], ident[:])
-            nc.scalar.activation(result[half][:, t0:t1], back[:, 0:width], ACT.Copy)
+            for b in range(0, PIECE, P):
+                nc.tensor.transpose(back[:, b : b + P], turned[:, first + b : first + b + P], ident[:])
+            nc.scalar.activation(result[half][:, t0 : t0 + PIECE], back[:, 0:PIECE], ACT.Copy)
 
-        for n, (half, t0) in enumerate([(0, 0), (0, 256), (1, 0), (1, 256), (0, 512), (0, 768)]):
+        for n, (half, t0) in enumerate(TENSOR_PIECES):
             piece = new_piece()
-            pick(piece, half, 0, t0, t0 + 256)
-            pick(piece, half, 1, t0, t0 + 256)
-            add_on_tensor(n, piece, half, t0, t0 + 256)
+            pick(piece, half, 0, t0, t0 + PIECE)
+            pick(piece, half, 1, t0, t0 + PIECE)
+            add_on_tensor(n, piece, half, t0)
             if n % 2 == 1:
-                store(half, t0 - 256, t0 + 256)
-        waiting = None
-        for t0, t1 in [(512, 768), (768, 896), (896, T)]:
-            if waiting is None:
-                piece = new_piece()
-                pick(piece, 1, 0, t0, t1)
-            else:
-                last = piece
-                piece = new_piece()
-                pick(piece, 1, 0, t0, t1)
-                add_on_vector(last, 1, *waiting)
-            pick(piece, 1, 1, t0, t1)
-            waiting = (t0, t1)
-        add_on_vector(piece, 1, *waiting)
-        store(1, 512, T)
+                store(nc.scalar, half, t0 - PIECE, t0 + PIECE)
+
+        long_piece = new_piece()
+        pick(long_piece, 1, 0, *LONG_PIECE)
+        pick(long_piece, 1, 1, *LONG_PIECE)
+        short_piece = new_piece()
+        pick(short_piece, 1, 0, *SHORT_PIECE)
+        add_on_vector(long_piece, *LONG_PIECE)
+        pick(short_piece, 1, 1, *SHORT_PIECE)
+        add_on_vector(short_piece, *SHORT_PIECE)
+        store(nc.sync, 1, LONG_PIECE[0], T)

from contextlib import ExitStack

import concourse.mybir as mybir
from concourse.masks import make_identity

K, T, E, C, H, N = 512, 1024, 8, 256, 512, 256
S = E * C
P = 128
PACK = 4
BANKS = 8
FLOPS = 2 * S * (K * H + H * N)

F32 = mybir.dt.float32
BF16 = mybir.dt.bfloat16
I32 = mybir.dt.int32
U32 = mybir.dt.uint32
U16 = mybir.dt.uint16
U8 = mybir.dt.uint8
FP8X4 = mybir.dt.float8_e4m3fn_x4
FP4X4 = mybir.dt.float4_e2m1fn_x4
ACT = mybir.ActivationFunctionType
ALU = mybir.AluOpType

X_CHUNKS = [(0, 512), (512, 768), (768, 1024)]
QUADRANTS = (0, 2, 1, 3)
PIECE = 256
TENSOR_PIECES = [(0, 0), (0, 256), (1, 0), (1, 256), (0, 512), (0, 768)]
LONG_PIECE = (512, 896)
SHORT_PIECE = (896, T)


def tile_moe_pln_mlp_gelu_kernel(
    tc, xT, w1_words, w1_scales, w2_words, w2_scales, gate, offs, pos1, pos2, out
):
    nc = tc.nc
    with ExitStack() as ctx:
        keep = ctx.enter_context(tc.tile_pool(name="keep", bufs=1))
        psum = ctx.enter_context(tc.psum_pool(name="psum", bufs=1))

        offs_sb = keep.tile([P, S // 16], U16, name="offs_sb")
        pos_sb = [keep.tile([P, T // 16], U16, name="pos1_sb"), keep.tile([P, T // 16], U16, name="pos2_sb")]
        s1_raw = keep.tile([P, H], U8, name="s1_raw", tag="after_s1", align_bytes=64)
        s1_perm = keep.tile([P, H], U8, name="s1_perm", align_bytes=64)
        s1 = keep.tile([P, E * H], U8, name="s1", align_bytes=64)
        w1 = keep.tile([P, E, 2 * H], U8, name="w1", align_bytes=64)
        x_raw = [
            keep.tile([P, PACK, t1 - t0], F32, name="x_raw", tag="after_x%d" % t0, align_bytes=64)
            for t0, t1 in X_CHUNKS
        ]
        x_bf = keep.tile([P, T * PACK], BF16, name="x_bf", align_bytes=64)
        x_codes = keep.tile([P, T], U32, name="x_codes", align_bytes=64)
        x_scales = keep.tile([P, T], U8, name="x_scales", align_bytes=64)
        slot_codes = keep.tile([P, S], U32, name="slot_codes", align_bytes=64)
        slot_scales = keep.tile([P, S], U8, name="slot_scales", align_bytes=64)
        h_bf = keep.tile([P, S * PACK], BF16, name="h_bf", align_bytes=64)
        h_codes = keep.tile([P, S], U32, name="h_codes", align_bytes=64)
        h_scales = keep.tile([P, S], U8, name="h_scales", align_bytes=64)
        y = [keep.tile([P, S], F32, name="y%d" % half) for half in range(2)]
        result = [keep.tile([P, T], F32, name="result%d" % half) for half in range(2)]
        turned = keep.tile([P, 2 * T], F32, name="turned")
        ident = keep.tile([P, P], F32, name="ident")
        warm = keep.tile([P, 16], F32, name="warm")

        nc.vector.memset(warm[:, 0:8], 0.0)
        nc.scalar.activation(warm[:, 8:16], warm[:, 0:8], ACT.Gelu_apprx_tanh)
        nc.vector.memset(x_scales[:].bitcast(I32), 0)
        make_identity(nc, ident[:])
        nc.vector.memset(s1[:].bitcast(I32), 0)

        w1_hbm = w1_words.rearrange("e s p b -> p (e s) b").bitcast(I32)
        x_hbm = xT.rearrange("(p j) t -> p j t", j=PACK)

        def load_w1(e0, e1):
            raw = keep.tile([P, e1 - e0, 2 * H], U8, name="w1_raw%d" % e0, align_bytes=64)
            nc.sync.dma_start(raw[:].bitcast(I32), w1_hbm[:, e0:e1, :])
            return raw

        def permute_w1(raw, e0, e1):
            nc.vector.tensor_copy(
                w1[:, e0:e1, :].bitcast(U16).rearrange("p e (d g m) -> p e g d m", d=PACK, m=8),
                raw[:, 0 : e1 - e0, :].bitcast(U16).rearrange("p e (g m d) -> p e g d m", d=PACK, m=8),
            )

        nc.sync.dma_start(s1_raw[:].bitcast(I32), w1_scales.rearrange("e s q i -> q (e s) i").bitcast(I32))
        w1_first = load_w1(0, E // 2)
        w1_second = load_w1(E // 2, E)
        for c, (t0, t1) in enumerate(X_CHUNKS):
            nc.sync.dma_start(x_raw[c][:], x_hbm[:, :, t0:t1])
        nc.sync.dma_start(offs_sb[:], offs)
        nc.sync.dma_start(pos_sb[0][:], pos1)
        nc.sync.dma_start(pos_sb[1][:], pos2)

        nc.vector.tensor_copy(
            s1_perm[:].rearrange("p (d m) -> p d m", d=PACK), s1_raw[:].rearrange("p (m d) -> p d m", d=PACK)
        )
        for quad in QUADRANTS:
            nc.sync.dma_start(
                s1[32 * quad : 32 * quad + 4, :].bitcast(I32), s1_perm[32 * quad : 32 * quad + 32, :].bitcast(I32)
            )
        permute_w1(w1_first, 0, E // 2)
        permute_w1(w1_second, E // 2, E)
        s2 = keep.tile([P, E * N], U8, name="s2", tag="after_s1", align_bytes=64)
        nc.vector.memset(s2[:].bitcast(I32), 0)
        s2_hbm = w2_scales.rearrange("e s q n -> q (e s) n").bitcast(I32)
        for quad in QUADRANTS:
            nc.sync.dma_start(
                s2[32 * quad : 32 * quad + 4, :].bitcast(I32).rearrange("p (e n) -> p e n", e=E),
                s2_hbm[4 * quad : 4 * quad + 4],
            )

        def cast_views(c, t0, t1):
            first = X_CHUNKS[c][0]
            dst = x_bf[:, (first + t0) * PACK : (first + t1) * PACK].rearrange("p (c i j) -> p c j i", i=4, j=PACK)
            src = x_raw[c][:, :, t0:t1].rearrange("p j (c i) -> p c j i", i=4)
            return dst, src

        def cast_on_scalar(c, t0, t1):
            dst, src = cast_views(c, t0, t1)
            nc.scalar.activation(dst, src, ACT.Copy)

        def cast_on_vector(c, t0, t1):
            dst, src = cast_views(c, t0, t1)
            nc.vector.tensor_copy(dst, src)

        def quantize_x(t0, t1):
            nc.vector.quantize_mx(
                out=x_codes[:, t0:t1].bitcast(FP8X4), scales=x_scales[:, t0:t1], in_=x_bf[:, t0 * PACK : t1 * PACK]
            )

        cast_on_scalar(0, 0, 256)
        cast_on_vector(0, 256, 512)
        quantize_x(256, 512)
        quantize_x(0, 256)
        cast_on_scalar(1, 0, 160)
        cast_on_vector(1, 160, 256)
        quantize_x(512, 768)
        cast_on_scalar(2, 0, 80)
        cast_on_vector(2, 128, 256)
        cast_on_vector(2, 80, 128)
        quantize_x(896, 1024)
        quantize_x(768, 896)

        w2 = keep.tile([P, E, 2 * N], U8, name="w2", tag="after_x0", align_bytes=64)
        nc.sync.dma_start(w2[:].bitcast(I32), w2_words.rearrange("e s p b -> p (e s) b").bitcast(I32))
        gate_hbm = gate.rearrange("r (h p) t -> p h r t", p=P)
        gate_sb = []
        for half in range(2):
            tile = keep.tile([P, 2, T], F32, name="gate_sb", tag="after_x%d" % X_CHUNKS[half + 1][0], align_bytes=64)
            nc.sync.dma_start(tile[:], gate_hbm[:, half])
            gate_sb.append(tile)

        def gather_slots(j0, j1):
            offsets = offs_sb[:, j0 // 16 : j1 // 16]
            nc.vector.tensor_copy(slot_codes[:, j0:j1], x_codes[:].indirect(offsets))
            nc.vector.tensor_copy(slot_scales[:, j0:j1], x_scales[:].indirect(offsets))

        def first_layer(j0):
            e = j0 // C
            bank = psum.tile([P, PACK, P], F32, name="bank%d" % (j0 // P % BANKS))
            for d in range(PACK):
                nc.tensor.matmul_mx(
                    out=bank[:, d, :],
                    lhsT=w1[:, e, 2 * P * d : 2 * P * (d + 1)].bitcast(FP4X4),
                    lhsT_scale=s1[:, e * H + P * d : e * H + P * (d + 1)],
                    rhs=slot_codes[:, j0 : j0 + P].bitcast(FP8X4),
                    rhs_scale=slot_scales[:, j0 : j0 + P],
                    start=True,
                    stop=True,
                )
            nc.scalar.activation(
                h_bf[:, j0 * PACK : (j0 + P) * PACK].rearrange("p (c d) -> p c d", d=PACK),
                bank[:].rearrange("p d c -> p c d"),
                ACT.Gelu_apprx_tanh,
            )

        def quantize_h(e0, e1):
            j0, j1 = e0 * C, e1 * C
            nc.vector.quantize_mx(
                out=h_codes[:, j0:j1].bitcast(FP8X4), scales=h_scales[:, j0:j1], in_=h_bf[:, j0 * PACK : j1 * PACK]
            )

        def second_layer(half, e0, e1, bank_number):
            bank = psum.tile([P, 2 * C], F32, name="bank%d" % bank_number)
            for e in range(e0, e1):
                nc.tensor.matmul_mx(
                    out=bank[:, (e - e0) * C : (e - e0 + 1) * C],
                    lhsT=w2[:, e, 2 * P * half : 2 * P * (half + 1)].bitcast(FP4X4),
                    lhsT_scale=s2[:, e * N + P * half : e * N + P * (half + 1)],
                    rhs=h_codes[:, e * C : (e + 1) * C].bitcast(FP8X4),
                    rhs_scale=h_scales[:, e * C : (e + 1) * C],
                    start=True,
                    stop=True,
                )
            return y[half][:, e0 * C : e1 * C], bank[:, 0 : (e1 - e0) * C]

        for e in range(E):
            gather_slots(e * C, (e + 1) * C)
            first_layer(e * C)
            first_layer(e * C + P)

        for bank_number, (e0, e1) in enumerate([(0, 2), (2, 4), (4, 6), (6, 7)]):
            quantize_h(e0, e1)
            dst, src = second_layer(0, e0, e1, bank_number)
            nc.scalar.activation(dst, src, ACT.Copy)
        quantize_h(E - 1, E)
        dst, src = second_layer(0, E - 1, E, 4)
        nc.vector.tensor_copy(dst, src)
        for pair in range(E // 2):
            dst, src = second_layer(1, 2 * pair, 2 * pair + 2, (5 + pair) % BANKS)
            nc.scalar.activation(dst, src, ACT.Copy)

        def new_piece():
            return keep.tile([P, 2, LONG_PIECE[1] - LONG_PIECE[0]], F32, name="picked", bufs=2)

        def pick(picked, half, r, t0, t1):
            nc.vector.tensor_tensor(
                picked[:, r, 0 : t1 - t0],
                y[half][:].indirect(pos_sb[r][:, t0 // 16 : t1 // 16]),
                gate_sb[half][:, r, t0:t1],
                ALU.mult,
            )

        def store(queue, half, t0, t1):
            queue.dma_start(out[half * P : (half + 1) * P, t0:t1], result[half][:, t0:t1])

        def add_on_vector(picked, t0, t1):
            nc.vector.tensor_tensor(result[1][:, t0:t1], picked[:, 0, 0 : t1 - t0], picked[:, 1, 0 : t1 - t0], ALU.add)

        def add_on_tensor(n, picked, half, t0):
            sums = psum.tile([P, PACK * P], F32, name="bank%d" % (1 + n % 2))
            for b in range(0, PIECE, P):
                for r in range(2):
                    nc.tensor.matmul(
                        sums[:, b : b + P],
                        lhsT=picked[:, r, b : b + P],
                        rhs=ident[:],
                        start=(r == 0),
                        stop=(r == 1),
                        is_transpose=True,
                    )
            first = half * T + t0
            nc.scalar.activation(turned[:, first : first + PIECE], sums[:, 0:PIECE], ACT.Copy)
            back = psum.tile([P, PACK * P], F32, name="bank%d" % (3 + n % 2))
            for b in range(0, PIECE, P):
                nc.tensor.transpose(back[:, b : b + P], turned[:, first + b : first + b + P], ident[:])
            nc.scalar.activation(result[half][:, t0 : t0 + PIECE], back[:, 0:PIECE], ACT.Copy)

        for n, (half, t0) in enumerate(TENSOR_PIECES):
            piece = new_piece()
            pick(piece, half, 0, t0, t0 + PIECE)
            pick(piece, half, 1, t0, t0 + PIECE)
            add_on_tensor(n, piece, half, t0)
            if n % 2 == 1:
                store(nc.scalar, half, t0 - PIECE, t0 + PIECE)

        long_piece = new_piece()
        pick(long_piece, 1, 0, *LONG_PIECE)
        pick(long_piece, 1, 1, *LONG_PIECE)
        short_piece = new_piece()
        pick(short_piece, 1, 0, *SHORT_PIECE)
        add_on_vector(long_piece, *LONG_PIECE)
        pick(short_piece, 1, 1, *SHORT_PIECE)
        add_on_vector(short_piece, *SHORT_PIECE)
        store(nc.sync, 1, LONG_PIECE[0], T)
